import numpy as np
import ml_dtypes


def mxq(x, axis, fmt="e4m3"):
    dtype, down = {"e4m3": (ml_dtypes.float8_e4m3fn, 7), "e5m2": (ml_dtypes.float8_e5m2, 14)}[fmt]
    v = np.moveaxis(np.asarray(x, np.float32).astype(ml_dtypes.bfloat16).astype(np.float64), axis, -1)
    blocks = v.reshape(v.shape[:-1] + (-1, 32))
    amax = np.abs(blocks).max(-1, keepdims=True)
    byte = np.maximum(np.where(amax > 0, np.frexp(amax)[1] - 1 + 127, 0) - down, 1)
    scale = np.exp2(byte - 127.0)
    codes = (blocks / scale).astype(np.float32).astype(dtype).astype(np.float64)
    return np.moveaxis((codes * scale).reshape(v.shape), -1, axis)


WIDE = False


def mx_kscale(k):
    if not WIDE:
        return np.ones(k)
    levels = np.array([10, -10, 5, -5, 0])
    if k % 512:
        return np.exp2(np.random.permutation(np.resize(levels, k // 32))).repeat(32)
    a = np.empty((k // 512, 16))
    for p in range(k // 512):
        a[p, :8] = np.random.permutation(np.resize(levels, 8))
        for g in range(8):
            far = levels[np.abs(levels - a[p, g]) >= 10]
            a[p, g + 8] = far[np.random.randint(len(far))]
    return np.exp2(a.ravel()).repeat(32)


BF16 = ml_dtypes.bfloat16


def bf(x):
    return np.asarray(x, np.float32).astype(BF16)


def f64(x):
    return np.asarray(x).astype(np.float64)


E2M1 = np.array([0.0, 0.5, 1.0, 1.5, 2.0, 3.0, 4.0, 6.0, -0.0, -0.5, -1.0, -1.5, -2.0, -3.0, -4.0, -6.0])


def pack_weight(w, fmt):
    k, n = w.shape
    w = f64(bf(w)).reshape(k // 32, 32, n)
    amax = np.abs(w).max(1)
    if fmt == "e4m3":
        byte = np.frexp(amax)[1] - 1 + 127 - 7
    else:
        mant, ex = np.frexp(amax / 6.0)
        byte = np.where(mant > 0.5, ex, ex - 1) + 127
    byte = np.clip(np.where(amax > 0, byte, 1), 1, 254)
    scaled = (w * np.exp2(127.0 - byte)[:, None, :]).reshape(k, n).astype(np.float32)
    by_word = np.ascontiguousarray(scaled.reshape(k // 512, 128, 4, n).transpose(0, 1, 3, 2))
    if fmt == "e4m3":
        words = by_word.astype(ml_dtypes.float8_e4m3fn).view(np.uint8)
    else:
        c = by_word.astype(ml_dtypes.float4_e2m1fn).view(np.uint8) & 0xF
        words = c[..., 0::2] | (c[..., 1::2] << 4)
    return np.ascontiguousarray(words), np.ascontiguousarray(byte.astype(np.uint8).reshape(k // 512, 16, n))


def unpack_weight(words, scales, fmt):
    g, p, n, _ = words.shape
    if fmt == "e4m3":
        vals = np.ascontiguousarray(words).view(ml_dtypes.float8_e4m3fn).astype(np.float64)
    else:
        nib = np.empty((g, p, n, 4), np.uint8)
        nib[..., 0::2] = words & 0xF
        nib[..., 1::2] = words >> 4
        vals = E2M1[nib]
    vals = vals * np.repeat(np.exp2(scales.astype(np.float64) - 127.0), 8, axis=1)[..., None]
    return vals.transpose(0, 1, 3, 2).reshape(g * 512, n)
def pack4(w):
    words, scales = pack_weight(w, "e2m1")
    return words.reshape(words.shape[0], 128, -1), scales


def unpack4(words, scales):
    return unpack_weight(words.reshape(words.shape[0], 128, -1, 2), scales, "e2m1")


E4M3FN = np.array([(-1.0 if i & 128 else 1.0) * ((1.0 + (i & 7) / 8.0) * 2.0 ** (((i >> 3) & 15) - 7) if i & 120 else (i & 7) * 2.0 ** -9) for i in range(256)])


def e4m3fn_bytes(y):
    return np.clip(np.asarray(y, np.float64), -448.0, 448.0).astype(np.float32).astype(ml_dtypes.float8_e4m3fn).view(np.uint8)


def e4m3fn_values(b):
    return E4M3FN[b]


N, D, H, E = 512, 1024, 4, 512
HE = H * E


def draw0():
    s, t = mx_kscale(D), mx_kscale(HE)
    x = bf((np.random.standard_normal((N, D)) + 0.5 * np.random.standard_normal((1, D))) * s[None, :])
    w_q_words, w_q_scales = pack4(np.random.standard_normal((D, HE)) / np.sqrt(D) / s[:, None])
    g_q = bf((1.0 + 0.1 * np.random.standard_normal(HE)) * t)
    w_k_words, w_k_scales = pack4(np.random.standard_normal((D, HE)) / np.sqrt(D) / s[:, None] / t[None, :])
    return {
        "x": x,
        "w_q_words": w_q_words,
        "w_q_scales": w_q_scales,
        "g_q": g_q,
        "w_k_words": w_k_words,
        "w_k_scales": w_k_scales,
        "w_head": bf(np.random.uniform(0.3, 0.8, H)),
        "b_head": bf(0.5 + 0.1 * np.random.standard_normal(1)),
    }


def attention_maps(q, k):
    qq = mxq(q.transpose(1, 0, 2), 2, "e4m3")
    kq = mxq(k.transpose(1, 2, 0), 1, "e4m3")
    logits = (qq @ kq) / np.sqrt(E)
    e = np.exp(logits - logits.max(axis=-1, keepdims=True))
    return e / e.sum(axis=-1, keepdims=True)


def average_product_correction(s):
    r = np.sum(s, axis=-1)
    t = np.sum(r, axis=-1)
    background = r[:, :, None] * r[:, None, :] / t[:, None, None]
    return s - background


def core(x, w_q_words, w_q_scales, g_q, w_k_words, w_k_scales, w_head, b_head):
    n = x.shape[0]
    heads = w_head.shape[0]
    xq = mxq(f64(x), 1, "e4m3")
    q = ((xq @ unpack4(w_q_words, w_q_scales)) * f64(g_q)[None, :]).reshape(n, heads, E)
    k = (xq @ unpack4(w_k_words, w_k_scales)).reshape(n, heads, E)
    a = attention_maps(q, k)
    s = a + np.swapaxes(a, -1, -2)
    c = average_product_correction(s)
    weights = n * f64(w_head)
    logit = f64(b_head)[0] + np.sum(weights[:, None, None] * c, axis=0)
    return 1.0 / (1.0 + np.exp(-logit))


def setup_inputs():
    drawn = draw0()
    full = np.asarray(drawn['x']).astype(np.float64)
    scale = (np.abs(full).reshape(512, 8, 128).max(axis=(2,)) / 448.0).astype(np.float32)
    given = {}
    for key, value in drawn.items():
        if key == 'x':
            given['x_bytes'] = e4m3fn_bytes(full / np.repeat(scale.astype(np.float64), 128, axis=1))
            given['x_scale'] = scale
        else:
            given[key] = value
    return given


def reference(x_bytes, x_scale, w_q_words, w_q_scales, g_q, w_k_words, w_k_scales, w_head, b_head):
    return core(e4m3fn_values(x_bytes) * np.repeat(x_scale.astype(np.float64), 128, axis=1), w_q_words, w_q_scales, g_q, w_k_words, w_k_scales, w_head, b_head)

@@ -1,0 +1,440 @@
+from contextlib import ExitStack
+
+import concourse.mybir as mybir
+from concourse.masks import make_identity
+
+P = 128
+N, D, H, E = 512, 1024, 4, 512
+FLOPS = 2 * 2 * N * D * H * E + H * 2 * N * N * E
+
+F32 = mybir.dt.float32
+BF16 = mybir.dt.bfloat16
+I32 = mybir.dt.int32
+U32 = mybir.dt.uint32
+U8 = mybir.dt.uint8
+F8 = mybir.dt.float8_e4m3fn
+F8X4 = mybir.dt.float8_e4m3fn_x4
+F4X4 = mybir.dt.float4_e2m1fn_x4
+ADD = mybir.AluOpType.add
+MULT = mybir.AluOpType.mult
+MIN = mybir.AluOpType.min
+ACT = mybir.ActivationFunctionType
+X = mybir.AxisListType.X
+SCALE = 1.0 / float(E) ** 0.5
+
+NT = N // P
+G = D // 512
+K_LEAD = 5
+Q_LEAD = 3
+V_BLOCKS = 5
+LAST = H - 1
+VIA_S = frozenset()
+Q_GAP = 1
+EARLY = False
+
+
+def tile_esmcontactheadapc_d1p_kernel(
+    tc, x_bytes, x_scale, w_q_words, w_q_scales, g_q, w_k_words, w_k_scales, w_head, b_head, out
+):
+    nc = tc.nc
+    with ExitStack() as ctx:
+        keep = ctx.enter_context(tc.tile_pool(name="keep", bufs=1))
+        work = ctx.enter_context(tc.tile_pool(name="work", bufs=3))
+        psum = ctx.enter_context(tc.psum_pool(name="psum", bufs=2))
+        ctx.enter_context(tc.manual_schedule())
+
+        def bank(tag):
+            t = psum.tile([P, 512], F32, name="bank_" + tag, tag=tag, bufs={"q": 2, "k": 2, "sc": 3, "cs": 1}[tag])
+            return t
+
+        def kept(name, shape, dt):
+            t = keep.tile(shape, dt, name=name, tag=name, align_bytes=64)
+            return t
+
+        x8 = [kept("x8_%d" % a, [P, D], U8) for a in range(NT)]
+        xs = kept("xs", [P, NT, 8], F32)
+        for a in range(NT):
+            nc.sync.dma_start(out=x8[a][:], in_=x_bytes[P * a : P * (a + 1), :])
+        nc.scalar.dma_start(out=xs[:], in_=x_scale.rearrange("(a p) j -> p a j", p=P))
+        raw_s = {}
+        raw_w = {}
+        words = {"q": w_q_words, "k": w_k_words}
+        scales = {"q": w_q_scales, "k": w_k_scales}
+        for w in ("k", "q"):
+            raw_s[w] = kept("raw_s_" + w, [P, G, H * E], U8)
+            nc.vector.memset(raw_s[w][:].bitcast(I32), 0)
+            for hp in range(2):
+                raw_w[w, hp] = kept("raw_w_%s%d" % (w, hp), [P, G, 2048], U8)
+
+        def load_scales(w):
+            for s in range(4):
+                nc.sync.dma_start(
+                    out=raw_s[w][32 * s : 32 * s + 4].bitcast(I32),
+                    in_=scales[w].bitcast(I32)[:, 4 * s : 4 * s + 4, :].rearrange("g s c -> s g c"),
+                )
+
+        def load_words(w, hp):
+            nc.sync.dma_start(
+                out=raw_w[w, hp][:].bitcast(I32),
+                in_=words[w].bitcast(I32)[:, :, 512 * hp : 512 * hp + 512].rearrange("g p c -> p g c"),
+            )
+
+        load_scales("k")
+        load_words("k", 0)
+        load_scales("q")
+        load_words("q", 0)
+        load_words("k", 1)
+        load_words("q", 1)
+
+        ident = kept("ident", [P, P], F32)
+        make_identity(nc, ident[:])
+        g_rows = kept("g_rows", [P, E], BF16)
+        nc.gpsimd.memset(g_rows[:], 0.0)
+        r_cols = kept("r_cols", [P, NT, P], F32)
+        nc.gpsimd.memset(r_cols[:], 0.0)
+        z_lhs = kept("z_lhs", [P, NT, P], F32)
+        nc.gpsimd.memset(z_lhs[:], 0.0)
+        nc.scalar.dma_start(out=g_rows[0:H, :], in_=g_q.rearrange("(h c) -> h c", h=H))
+        w_b = kept("w_b", [P, H], BF16)
+        nc.scalar.dma_start(out=w_b[:], in_=w_head.partition_broadcast(P))
+        b_b = kept("b_b", [P, 1], BF16)
+        nc.scalar.dma_start(out=b_b[:], in_=b_head.partition_broadcast(P))
+
+        perm_w = {}
+        perm_s = {}
+
+        def permute_scales(w):
+            perm_s[w] = kept("perm_s_" + w, [P, G * H * E], U8)
+            nc.vector.tensor_copy(
+                out=perm_s[w][:].bitcast(I32).rearrange("p (t q b) -> p t q b", t=4, b=2),
+                in_=raw_s[w][:].rearrange("p g c -> p (g c)").bitcast(I32).rearrange("p (q t b) -> p t q b", t=4, b=2),
+            )
+
+        def permute_words(w, hp):
+            perm_w[w, hp] = kept("perm_w_%s%d" % (w, hp), [P, G * 2048], U8)
+            nc.vector.tensor_copy(
+                out=perm_w[w, hp][:].bitcast(I32).rearrange("p (t q b) -> p t q b", t=4, b=4),
+                in_=raw_w[w, hp][:].rearrange("p g c -> p (g c)").bitcast(I32).rearrange("p (q t b) -> p t q b", t=4, b=4),
+            )
+
+        xb = [kept("xb_%d" % a, [P, D], BF16) for a in range(NT)]
+        xt = [kept("xt_%d" % a, [P, G, P, 4], BF16) for a in range(NT)]
+        xq = [kept("xq_%d" % a, [P, G * P], U32) for a in range(NT)]
+        xq_s = [kept("xqs_%d" % a, [P, G * P], U8) for a in range(NT)]
+
+        def widen(a):
+            for c in range(8):
+                cols = slice(P * c, P * (c + 1))
+                src = x8[a][:, cols].bitcast(F8)
+                if c < V_BLOCKS:
+                    nc.vector.tensor_scalar(
+                        out=xb[a][:, cols], in0=src, scalar1=xs[:, a, c : c + 1], scalar2=None, op0=MULT
+                    )
+                else:
+                    nc.scalar.activation(out=xb[a][:, cols], in_=src, func=ACT.Copy, scale=xs[:, a, c : c + 1])
+
+        def turn(a):
+            ps = bank("q" if a % 2 == 0 else "k")
+            w32 = xb[a][:].bitcast(F32)
+            for g in range(G):
+                for u in range(2):
+                    s = 2 * g + u
+                    nc.tensor.transpose(
+                        ps[:, P * s : P * (s + 1)], w32[:, 256 * g + u : 256 * (g + 1) : 2], ident[:]
+                    )
+            return ps
+
+        def turned_out(a, ps):
+            nc.scalar.copy(
+                out=xt[a][:].rearrange("p g r t -> p (g r t)").bitcast(F32).rearrange("p (g r u) -> p g r u", g=G, u=2),
+                in_=ps[:].rearrange("p (g u r) -> p g r u", g=G, u=2),
+            )
+
+        def quant_x(a):
+            nc.vector.quantize_mx(
+                out=xq[a][:].bitcast(F8X4), scales=xq_s[a][:], in_=xt[a][:].rearrange("p g r t -> p (g r t)")
+            )
+
+        g_perm = kept("g_perm", [P, 4, P], F32)
+        g_cols = kept("g_cols", [P, H, 4], F32)
+
+        def gain_rows():
+            nc.vector.tensor_copy(
+                out=g_perm[:].rearrange("p t (q b) -> p t q b", b=8),
+                in_=g_rows[:].rearrange("p (q t b) -> p t q b", t=4, b=8),
+            )
+
+        def gain_columns():
+            psg = bank("sc")
+            for t in range(4):
+                nc.tensor.transpose(psg[:, P * t : P * (t + 1)], g_perm[:, t, :], ident[:])
+            nc.vector.tensor_copy(out=g_cols[:], in_=psg[:].rearrange("p (t m) -> p m t", t=4)[:, 0:H, :])
+
+        w512 = kept("w512", [P, H], F32)
+        w_pick = kept("w_pick", [P, H], F32)
+        one_col = kept("one_col", [P, 1], F32)
+        w_col = kept("w_col", [P, 1], F32)
+        w_half = kept("w_half", [P, 1], F32)
+
+        def head_weights():
+            nc.vector.tensor_scalar(out=w512[:], in0=w_b[:], scalar1=float(N), scalar2=None, op0=MULT)
+            nc.vector.tensor_tensor(out=w_pick[:], in0=ident[:, 0:H], in1=w_b[:], op=MULT)
+            nc.vector.tensor_reduce(out=one_col[:], in_=ident[:, 0:H], axis=X, op=ADD)
+            nc.vector.tensor_reduce(out=w_col[:], in_=w_pick[:], axis=X, op=ADD)
+            nc.vector.tensor_scalar(out=w_half[:], in0=w_col[:], scalar1=-0.5, scalar2=None, op0=MULT)
+
+        dummy = kept("dummy", [P, 1], F32)
+        nc.scalar.activation(out=dummy[:], in_=ident[:, 0:1], func=ACT.Exp)
+        widen(0)
+        widen(1)
+        ps0 = turn(0)
+        turned_out(0, ps0)
+        widen(2)
+        ps1 = turn(1)
+        turned_out(1, ps1)
+        quant_x(0)
+        widen(3)
+        permute_scales("k")
+        quant_x(1)
+        permute_words("k", 0)
+        ps2 = turn(2)
+        turned_out(2, ps2)
+        ps3 = turn(3)
+        turned_out(3, ps3)
+        quant_x(2)
+        quant_x(3)
+        permute_scales("q")
+        gain_rows()
+        permute_words("q", 0)
+
+        unit_ps = {}
+        raw = {}
+        codes = {}
+        plane = {}
+
+        def project(w, m):
+            h, nb = divmod(m, NT)
+            hp, hh = divmod(h, 2)
+            ps = bank(w)
+            unit_ps[w, m] = ps
+            for t in range(4):
+                for g in range(G):
+                    o = t * 1024 + g * 512 + hh * 256
+                    so = t * 1024 + g * 512 + h * 128
+                    nc.tensor.matmul_mx(
+                        out=ps[:, P * t : P * (t + 1)],
+                        lhsT=perm_w[w, hp][:, o : o + 256].bitcast(F4X4),
+                        lhsT_scale=perm_s[w][:, so : so + P],
+                        rhs=xq[nb][:, P * g : P * (g + 1)].bitcast(F8X4),
+                        rhs_scale=xq_s[nb][:, P * g : P * (g + 1)],
+                        start=(g == 0),
+                        stop=(g == G - 1),
+                    )
+
+        def copy_q(m):
+            h = m // NT
+            r = work.tile([P, P, 4], BF16, name="q_raw", tag="q_raw", bufs=3, align_bytes=64)
+            raw["q", m] = r
+            if m in VIA_S:
+                flat = work.tile([P, 4, P], BF16, name="q_flat", tag="q_flat", bufs=2, align_bytes=64)
+                for t in range(4):
+                    nc.scalar.activation(
+                        out=flat[:, t, :],
+                        in_=unit_ps["q", m][:, P * t : P * (t + 1)],
+                        func=ACT.Copy,
+                        scale=g_cols[:, h, t : t + 1],
+                    )
+                flat_q[m] = flat
+                return
+            nc.vector.tensor_tensor(
+                out=r[:],
+                in0=unit_ps["q", m][:].rearrange("p (t n) -> p n t", t=4),
+                in1=g_cols[:, h, :].unsqueeze(1).to_broadcast([P, P, 4]),
+                op=MULT,
+            )
+
+        flat_q = {}
+
+        def interleave_q(m):
+            if m in VIA_S:
+                nc.vector.tensor_copy(out=raw["q", m][:], in_=flat_q[m][:].rearrange("p t n -> p n t"))
+
+        def copy_k(m):
+            r = work.tile([P, P, 4], BF16, name="k_raw", tag="k_raw", bufs=3, align_bytes=64)
+            raw["k", m] = r
+            nc.scalar.copy(out=r[:], in_=unit_ps["k", m][:].rearrange("p (t n) -> p n t", t=4))
+
+        def quant(w, m):
+            h, nb = divmod(m, NT)
+            if nb == 0:
+                c = work.tile([P, N], U32, name="codes_" + w, tag="codes_" + w, bufs=3, align_bytes=64)
+                s = work.tile([P, N], U8, name="plane_" + w, tag="plane_" + w, bufs=3, align_bytes=64)
+                codes[w, h] = c
+                plane[w, h] = s
+            cols = slice(P * nb, P * (nb + 1))
+            nc.vector.quantize_mx(
+                out=codes[w, h][:, cols].bitcast(F8X4),
+                scales=plane[w, h][:, cols],
+                in_=raw[w, m][:].rearrange("p n t -> p (n t)"),
+            )
+
+        sc = {}
+        bias = {}
+        e_of = {}
+        z_of = {}
+        rz = {}
+        coef = {}
+        acc = [kept("acc_%d" % i, [P, N], F32) for i in range(NT)]
+        col_ps = {}
+
+        def score(n):
+            h, i = divmod(n, NT)
+            ps = bank("sc")
+            sc[n] = ps
+            cols = slice(P * i, P * (i + 1))
+            nc.tensor.matmul_mx(
+                out=ps[:],
+                lhsT=codes["q", h][:, cols].bitcast(F8X4),
+                lhsT_scale=plane["q", h][:, cols],
+                rhs=codes["k", h][:].bitcast(F8X4),
+                rhs_scale=plane["k", h][:],
+                start=True,
+                stop=True,
+            )
+
+        def row_max(n):
+            trash = work.tile([P, N], BF16, name="trash", tag="trash", bufs=1)
+            b = work.tile([P, 1], F32, name="bias", tag="bias", bufs=4)
+            bias[n] = b
+            nc.vector.tensor_scalar(
+                out=trash[:], in0=sc[n][:], scalar1=-SCALE, scalar2=None, op0=MULT, op1=MIN, accum_out=b[:]
+            )
+
+        def expo(n):
+            e = work.tile([P, N], F32, name="e", tag="e", bufs=4)
+            z = work.tile([P, 1], F32, name="z", tag="z", bufs=4)
+            e_of[n] = e
+            z_of[n] = z
+            nc.scalar.activation(out=e[:], in_=sc[n][:], func=ACT.Exp, bias=bias[n][:], scale=SCALE, accum_out=z[:])
+
+        def recip(n):
+            h, i = divmod(n, NT)
+            if h == LAST:
+                r = z_lhs[:, i, h : h + 1]
+            else:
+                r_tile = work.tile([P, 1], F32, name="rz", tag="rz", bufs=4)
+                r = r_tile[:]
+            rz[n] = r
+            nc.vector.reciprocal(out=r, in_=z_of[n][:])
+            c = work.tile([P, 1], F32, name="coef", tag="coef", bufs=4)
+            coef[n] = c
+            nc.gpsimd.tensor_tensor(out=c[:], in0=r, in1=w512[:, h : h + 1], op=MULT)
+
+        def accumulate(n):
+            h, i = divmod(n, NT)
+            if h == 0:
+                nc.scalar.activation(out=acc[i][:], in_=e_of[n][:], func=ACT.Copy, scale=coef[n][:])
+            else:
+                nc.vector.scalar_tensor_tensor(
+                    out=acc[i][:], in0=e_of[n][:], scalar=coef[n][:], in1=acc[i][:], op0=MULT, op1=ADD
+                )
+
+        def transpose_add(dst, src, start, stop):
+            nc.tensor.matmul(dst, lhsT=src, rhs=ident[:], is_transpose=True, start=start, stop=stop)
+
+        def col_sums(n):
+            h, i = divmod(n, NT)
+            if i == 0:
+                col_ps[h] = bank("cs")
+            for j in range(NT):
+                nc.tensor.matmul(
+                    col_ps[h][:, j : j + 1],
+                    lhsT=e_of[n][:, P * j : P * (j + 1)],
+                    rhs=rz[n],
+                    start=(i == 0 and j == 0),
+                    stop=(i == NT - 1 and j == NT - 1),
+                )
+            if i == NT - 1:
+                nc.vector.tensor_copy(out=r_cols[:, :, h], in_=col_ps[h][:, 0:NT])
+
+        def col_sums_last(n):
+            i = n % NT
+            if i == 0:
+                col_ps[LAST] = bank("cs")
+            nc.tensor.matmul(col_ps[LAST][:], lhsT=z_lhs[:, i, :], rhs=e_of[n][:], start=(i == 0), stop=(i == NT - 1))
+            if i == 0:
+                for j in range(NT):
+                    transpose_add(col_ps[LAST][:, P * j : P * (j + 1)], r_cols[:, j, :], False, False)
+
+        tiles = H * NT
+        for n in range(-K_LEAD, tiles + 1):
+            if 0 <= n + K_LEAD < tiles:
+                project("k", n + K_LEAD)
+            if n == -4:
+                gain_columns()
+            if n == -3:
+                head_weights()
+            if 0 <= n + Q_LEAD < tiles:
+                project("q", n + Q_LEAD)
+            if 0 <= n + K_LEAD - 1 < tiles:
+                copy_k(n + K_LEAD - 1)
+            if 0 <= n + Q_LEAD - 1 < tiles:
+                copy_q(n + Q_LEAD - 1)
+            if 0 <= n + Q_LEAD - Q_GAP < tiles:
+                interleave_q(n + Q_LEAD - Q_GAP)
+            if 0 <= n - 1 < tiles:
+                recip(n - 1)
+            if 0 <= n < tiles:
+                row_max(n)
+            if 0 <= n + K_LEAD - 1 < tiles:
+                quant("k", n + K_LEAD - 1)
+            if 0 <= n + Q_LEAD - Q_GAP < tiles:
+                quant("q", n + Q_LEAD - Q_GAP)
+            if 0 <= n < tiles:
+                expo(n)
+            if n == -2:
+                permute_words("k", 1)
+            if n == 1:
+                permute_words("q", 1)
+            if 0 <= n + 1 < tiles and EARLY:
+                score(n + 1)
+            if 0 <= n - 1 < LAST * NT:
+                col_sums(n - 1)
+            if n == tiles - 2:
+                col_sums_last(n - 2)
+            if n >= tiles - 2:
+                col_sums_last(n - 1)
+            if 0 <= n + 1 < tiles and not EARLY:
+                score(n + 1)
+            if 0 <= n - 1 < tiles:
+                accumulate(n - 1)
+
+        dummy2 = kept("dummy2", [P, 1], F32)
+        nc.scalar.activation(out=dummy2[:], in_=ident[:, 0:1], func=ACT.Sigmoid)
+        r_row = kept("r_row", [P, N], F32)
+        wr_row = kept("wr_row", [P, N], F32)
+        nc.vector.tensor_scalar(out=r_row[:], in0=col_ps[LAST][:], scalar1=one_col[:], scalar2=None, op0=ADD)
+        nc.vector.tensor_scalar(out=wr_row[:], in0=r_row[:], scalar1=w_half[:], scalar2=None, op0=MULT)
+        po = [bank("q" if i % 2 == 0 else "k") for i in range(NT)]
+        for i in range(NT):
+            for j in range(i, NT):
+                transpose_add(po[i][:, P * j : P * (j + 1)], acc[j][:, P * i : P * (i + 1)], j == i, False)
+        sg = [kept("sg_%d" % i, [P, N], F32) for i in range(NT)]
+        mirror = {}
+        for i in range(1, NT):
+            mirror[i] = bank("sc")
+        for i in range(NT):
+            rows = slice(P * i, P * (i + 1))
+            right = slice(P * i, N)
+            nc.tensor.matmul(po[i][:, right], lhsT=wr_row[:, rows], rhs=r_row[:, right], start=False, stop=True)
+        for i in range(NT):
+            rows = slice(P * i, P * (i + 1))
+            right = slice(P * i, N)
+            lg = work.tile([P, N], F32, name="lg", tag="lg", bufs=4)
+            nc.vector.tensor_tensor(out=lg[:, right], in0=po[i][:, right], in1=acc[i][:, right], op=ADD)
+            nc.scalar.activation(out=sg[i][:, right], in_=lg[:, right], func=ACT.Sigmoid, bias=b_b[:], scale=1.0)
+            for j in range(i + 1, NT):
+                nc.tensor.transpose(mirror[j][:, rows], sg[i][:, P * j : P * (j + 1)], ident[:])
+            if i > 0:
+                nc.vector.tensor_copy(out=sg[i][:, 0 : P * i], in_=mirror[i][:, 0 : P * i])
+            nc.sync.dma_start(out=out[rows, :], in_=sg[i][:])

@@ -18,6 +18,7 @@ F4X4 = mybir.dt.float4_e2m1fn_x4
 ADD = mybir.AluOpType.add
 MULT = mybir.AluOpType.mult
 MIN = mybir.AluOpType.min
+MAX = mybir.AluOpType.max
 ACT = mybir.ActivationFunctionType
 X = mybir.AxisListType.X
 SCALE = 1.0 / float(E) ** 0.5
@@ -31,6 +32,12 @@ LAST = H - 1
 VIA_S = frozenset()
 Q_GAP = 1
 EARLY = False
+NEG_ON_S = True
+PAIR_K = True
+ACC0_ON_S = False
+C_LAG = 2
+WARM = 4
+WARM2 = 0
 
 
 def tile_esmcontactheadapc_d1p_kernel(
@@ -41,7 +48,6 @@ def tile_esmcontactheadapc_d1p_kernel(
         keep = ctx.enter_context(tc.tile_pool(name="keep", bufs=1))
         work = ctx.enter_context(tc.tile_pool(name="work", bufs=3))
         psum = ctx.enter_context(tc.psum_pool(name="psum", bufs=2))
-        ctx.enter_context(tc.manual_schedule())
 
         def bank(tag):
             t = psum.tile([P, 512], F32, name="bank_" + tag, tag=tag, bufs={"q": 2, "k": 2, "sc": 3, "cs": 1}[tag])
@@ -51,11 +57,30 @@ def tile_esmcontactheadapc_d1p_kernel(
             t = keep.tile(shape, dt, name=name, tag=name, align_bytes=64)
             return t
 
+        zero = kept("zero", [P, N], BF16)
+        nc.vector.memset(zero[:], 0.0)
+        dummy = kept("dummy", [P, 1], F32)
+        nc.scalar.activation(out=dummy[:], in_=zero[:, 0:1], func=ACT.Exp)
+
+        def warm(count):
+            for c in range(count):
+                nc.tensor.matmul(bank("sc")[:], lhsT=zero[:, 0:P], rhs=zero[:], start=True, stop=True)
+
+        warm(WARM)
         x8 = [kept("x8_%d" % a, [P, D], U8) for a in range(NT)]
         xs = kept("xs", [P, NT, 8], F32)
+        nc.sync.dma_start(out=xs[:], in_=x_scale.rearrange("(a p) j -> p a j", p=P))
         for a in range(NT):
             nc.sync.dma_start(out=x8[a][:], in_=x_bytes[P * a : P * (a + 1), :])
-        nc.scalar.dma_start(out=xs[:], in_=x_scale.rearrange("(a p) j -> p a j", p=P))
+        g_rows = kept("g_rows", [P, E], BF16)
+        w_b = kept("w_b", [P, H], BF16)
+        b_b = kept("b_b", [P, 1], BF16)
+        nc.gpsimd.memset(g_rows[:], 0.0)
+        nc.gpsimd.dma_start(out=g_rows[0:H, :], in_=g_q.rearrange("(h c) -> h c", h=H))
+        ident = kept("ident", [P, P], F32)
+        make_identity(nc, ident[:])
+        nc.gpsimd.dma_start(out=w_b[:], in_=w_head.partition_broadcast(P))
+        nc.gpsimd.dma_start(out=b_b[:], in_=b_head.partition_broadcast(P))
         raw_s = {}
         raw_w = {}
         words = {"q": w_q_words, "k": w_k_words}
@@ -86,19 +111,10 @@ def tile_esmcontactheadapc_d1p_kernel(
         load_words("k", 1)
         load_words("q", 1)
 
-        ident = kept("ident", [P, P], F32)
-        make_identity(nc, ident[:])
-        g_rows = kept("g_rows", [P, E], BF16)
-        nc.gpsimd.memset(g_rows[:], 0.0)
         r_cols = kept("r_cols", [P, NT, P], F32)
         nc.gpsimd.memset(r_cols[:], 0.0)
         z_lhs = kept("z_lhs", [P, NT, P], F32)
         nc.gpsimd.memset(z_lhs[:], 0.0)
-        nc.scalar.dma_start(out=g_rows[0:H, :], in_=g_q.rearrange("(h c) -> h c", h=H))
-        w_b = kept("w_b", [P, H], BF16)
-        nc.scalar.dma_start(out=w_b[:], in_=w_head.partition_broadcast(P))
-        b_b = kept("b_b", [P, 1], BF16)
-        nc.scalar.dma_start(out=b_b[:], in_=b_head.partition_broadcast(P))
 
         perm_w = {}
         perm_s = {}
@@ -142,6 +158,7 @@ def tile_esmcontactheadapc_d1p_kernel(
                     nc.tensor.transpose(
                         ps[:, P * s : P * (s + 1)], w32[:, 256 * g + u : 256 * (g + 1) : 2], ident[:]
                     )
+            warm(WARM2)
             return ps
 
         def turned_out(a, ps):
@@ -183,8 +200,6 @@ def tile_esmcontactheadapc_d1p_kernel(
             nc.vector.tensor_reduce(out=w_col[:], in_=w_pick[:], axis=X, op=ADD)
             nc.vector.tensor_scalar(out=w_half[:], in0=w_col[:], scalar1=-0.5, scalar2=None, op0=MULT)
 
-        dummy = kept("dummy", [P, 1], F32)
-        nc.scalar.activation(out=dummy[:], in_=ident[:, 0:1], func=ACT.Exp)
         widen(0)
         widen(1)
         ps0 = turn(0)
@@ -260,18 +275,33 @@ def tile_esmcontactheadapc_d1p_kernel(
                 nc.vector.tensor_copy(out=raw["q", m][:], in_=flat_q[m][:].rearrange("p t n -> p n t"))
 
         def copy_k(m):
+            if PAIR_K:
+                if m % 2 == 0:
+                    pair = work.tile([P, 2 * P, 4], BF16, name="k_raw", tag="k_raw", bufs=2, align_bytes=64)
+                    raw["k", m] = pair
+                else:
+                    raw["k", m] = raw["k", m - 1]
+                half = P * (m % 2)
+                nc.scalar.copy(
+                    out=raw["k", m][:, half : half + P, :], in_=unit_ps["k", m][:].rearrange("p (t n) -> p n t", t=4)
+                )
+                return
             r = work.tile([P, P, 4], BF16, name="k_raw", tag="k_raw", bufs=3, align_bytes=64)
             raw["k", m] = r
             nc.scalar.copy(out=r[:], in_=unit_ps["k", m][:].rearrange("p (t n) -> p n t", t=4))
 
         def quant(w, m):
             h, nb = divmod(m, NT)
-            if nb == 0:
+            if w == "k" and PAIR_K and nb % 2 == 0:
+                return
+            if nb == (1 if w == "k" and PAIR_K else 0):
                 c = work.tile([P, N], U32, name="codes_" + w, tag="codes_" + w, bufs=3, align_bytes=64)
                 s = work.tile([P, N], U8, name="plane_" + w, tag="plane_" + w, bufs=3, align_bytes=64)
                 codes[w, h] = c
                 plane[w, h] = s
             cols = slice(P * nb, P * (nb + 1))
+            if w == "k" and PAIR_K:
+                cols = slice(P * (nb - 1), P * (nb + 1))
             nc.vector.quantize_mx(
                 out=codes[w, h][:, cols].bitcast(F8X4),
                 scales=plane[w, h][:, cols],
@@ -284,6 +314,7 @@ def tile_esmcontactheadapc_d1p_kernel(
         z_of = {}
         rz = {}
         coef = {}
+        a_of = {}
         acc = [kept("acc_%d" % i, [P, N], F32) for i in range(NT)]
         col_ps = {}
 
@@ -303,12 +334,23 @@ def tile_esmcontactheadapc_d1p_kernel(
             )
 
         def row_max(n):
-            trash = work.tile([P, N], BF16, name="trash", tag="trash", bufs=1)
             b = work.tile([P, 1], F32, name="bias", tag="bias", bufs=4)
             bias[n] = b
+            if NEG_ON_S:
+                mx = work.tile([P, 1], F32, name="mx", tag="mx", bufs=4)
+                nc.vector.tensor_reduce(out=mx[:], in_=sc[n][:], axis=X, op=MAX)
+                mx_of[n] = mx
+                return
+            trash = work.tile([P, N], BF16, name="trash", tag="trash", bufs=1)
             nc.vector.tensor_scalar(
                 out=trash[:], in0=sc[n][:], scalar1=-SCALE, scalar2=None, op0=MULT, op1=MIN, accum_out=b[:]
             )
+
+        mx_of = {}
+
+        def bias_of(n):
+            if NEG_ON_S:
+                nc.scalar.activation(out=bias[n][:], in_=mx_of[n][:], func=ACT.Copy, scale=-SCALE)
 
         def expo(n):
             e = work.tile([P, N], F32, name="e", tag="e", bufs=4)
@@ -326,17 +368,33 @@ def tile_esmcontactheadapc_d1p_kernel(
                 r = r_tile[:]
             rz[n] = r
             nc.vector.reciprocal(out=r, in_=z_of[n][:])
-            c = work.tile([P, 1], F32, name="coef", tag="coef", bufs=4)
-            coef[n] = c
-            nc.gpsimd.tensor_tensor(out=c[:], in0=r, in1=w512[:, h : h + 1], op=MULT)
+            if h == LAST:
+                c = work.tile([P, 1], F32, name="coef", tag="coef", bufs=4)
+                coef[n] = c
+                nc.gpsimd.tensor_tensor(out=c[:], in0=r, in1=w512[:, h : h + 1], op=MULT)
+
+        def norm(n):
+            if n // NT == LAST:
+                return
+            a = work.tile([P, N], F32, name="a", tag="a", bufs=4)
+            a_of[n] = a
+            nc.scalar.activation(out=a[:], in_=e_of[n][:], func=ACT.Copy, scale=rz[n])
 
         def accumulate(n):
             h, i = divmod(n, NT)
             if h == 0:
-                nc.scalar.activation(out=acc[i][:], in_=e_of[n][:], func=ACT.Copy, scale=coef[n][:])
+                if ACC0_ON_S:
+                    nc.scalar.activation(out=acc[i][:], in_=a_of[n][:], func=ACT.Copy, scale=w512[:, 0:1])
+                else:
+                    nc.vector.tensor_scalar(out=acc[i][:], in0=a_of[n][:], scalar1=w512[:, 0:1], scalar2=None, op0=MULT)
             else:
                 nc.vector.scalar_tensor_tensor(
-                    out=acc[i][:], in0=e_of[n][:], scalar=coef[n][:], in1=acc[i][:], op0=MULT, op1=ADD
+                    out=acc[i][:],
+                    in0=(e_of if h == LAST else a_of)[n][:],
+                    scalar=coef[n][:] if h == LAST else w512[:, h : h + 1],
+                    in1=acc[i][:],
+                    op0=MULT,
+                    op1=ADD,
                 )
 
         def transpose_add(dst, src, start, stop):
@@ -347,15 +405,13 @@ def tile_esmcontactheadapc_d1p_kernel(
             if i == 0:
                 col_ps[h] = bank("cs")
             for j in range(NT):
-                nc.tensor.matmul(
-                    col_ps[h][:, j : j + 1],
-                    lhsT=e_of[n][:, P * j : P * (j + 1)],
-                    rhs=rz[n],
-                    start=(i == 0 and j == 0),
-                    stop=(i == NT - 1 and j == NT - 1),
-                )
-            if i == NT - 1:
-                nc.vector.tensor_copy(out=r_cols[:, :, h], in_=col_ps[h][:, 0:NT])
+                cols = slice(P * j, P * (j + 1))
+                transpose_add(col_ps[h][:, cols], a_of[n][:, cols], i == 0 and j == 0, i == NT - 1 and j == NT - 1)
+
+        def col_reduce(h):
+            nc.vector.tensor_reduce(
+                out=r_cols[:, :, h], in_=col_ps[h][:].rearrange("p (j i) -> p j i", j=NT), axis=X, op=ADD
+            )
 
         def col_sums_last(n):
             i = n % NT
@@ -376,45 +432,50 @@ def tile_esmcontactheadapc_d1p_kernel(
                 head_weights()
             if 0 <= n + Q_LEAD < tiles:
                 project("q", n + Q_LEAD)
-            if 0 <= n + K_LEAD - 1 < tiles:
-                copy_k(n + K_LEAD - 1)
-            if 0 <= n + Q_LEAD - 1 < tiles:
-                copy_q(n + Q_LEAD - 1)
-            if 0 <= n + Q_LEAD - Q_GAP < tiles:
-                interleave_q(n + Q_LEAD - Q_GAP)
-            if 0 <= n - 1 < tiles:
-                recip(n - 1)
             if 0 <= n < tiles:
                 row_max(n)
+            if 0 <= n - 1 < tiles:
+                recip(n - 1)
+            if 0 <= n + K_LEAD - 1 < tiles:
+                copy_k(n + K_LEAD - 1)
+            if 0 <= n < tiles:
+                bias_of(n)
+            if 0 <= n - 1 < tiles:
+                norm(n - 1)
+            if 0 <= n + Q_LEAD - 1 < tiles:
+                copy_q(n + Q_LEAD - 1)
+            if 0 <= n < tiles:
+                expo(n)
+            if 0 <= n + Q_LEAD - Q_GAP < tiles:
+                interleave_q(n + Q_LEAD - Q_GAP)
             if 0 <= n + K_LEAD - 1 < tiles:
                 quant("k", n + K_LEAD - 1)
             if 0 <= n + Q_LEAD - Q_GAP < tiles:
                 quant("q", n + Q_LEAD - Q_GAP)
-            if 0 <= n < tiles:
-                expo(n)
             if n == -2:
                 permute_words("k", 1)
             if n == 1:
                 permute_words("q", 1)
-            if 0 <= n + 1 < tiles and EARLY:
+            if 0 <= n - C_LAG < LAST * NT:
+                col_sums(n - C_LAG)
+                if (n - C_LAG) % NT == NT - 1:
+                    col_reduce((n - C_LAG) // NT)
+            if 0 <= n + 1 < tiles:
                 score(n + 1)
-            if 0 <= n - 1 < LAST * NT:
-                col_sums(n - 1)
             if n == tiles - 2:
                 col_sums_last(n - 2)
             if n >= tiles - 2:
                 col_sums_last(n - 1)
-            if 0 <= n + 1 < tiles and not EARLY:
-                score(n + 1)
             if 0 <= n - 1 < tiles:
                 accumulate(n - 1)
 
         dummy2 = kept("dummy2", [P, 1], F32)
-        nc.scalar.activation(out=dummy2[:], in_=ident[:, 0:1], func=ACT.Sigmoid)
+        nc.scalar.activation(out=dummy2[:], in_=z_of[tiles - 1][:], func=ACT.Sigmoid)
         r_row = kept("r_row", [P, N], F32)
         wr_row = kept("wr_row", [P, N], F32)
         nc.vector.tensor_scalar(out=r_row[:], in0=col_ps[LAST][:], scalar1=one_col[:], scalar2=None, op0=ADD)
-        nc.vector.tensor_scalar(out=wr_row[:], in0=r_row[:], scalar1=w_half[:], scalar2=None, op0=MULT)
+        for part in (slice(0, P), slice(P, N)):
+            nc.vector.tensor_scalar(out=wr_row[:, part], in0=r_row[:, part], scalar1=w_half[:], scalar2=None, op0=MULT)
         po = [bank("q" if i % 2 == 0 else "k") for i in range(NT)]
         for i in range(NT):
             for j in range(i, NT):

from contextlib import ExitStack

import concourse.mybir as mybir
from concourse.masks import make_identity

P = 128
N, D, H, E = 512, 1024, 4, 512
FLOPS = 2 * 2 * N * D * H * E + H * 2 * N * N * E

F32 = mybir.dt.float32
BF16 = mybir.dt.bfloat16
I32 = mybir.dt.int32
U32 = mybir.dt.uint32
U8 = mybir.dt.uint8
F8 = mybir.dt.float8_e4m3fn
F8X4 = mybir.dt.float8_e4m3fn_x4
F4X4 = mybir.dt.float4_e2m1fn_x4
ADD = mybir.AluOpType.add
MULT = mybir.AluOpType.mult
MIN = mybir.AluOpType.min
MAX = mybir.AluOpType.max
ACT = mybir.ActivationFunctionType
X = mybir.AxisListType.X
SCALE = 1.0 / float(E) ** 0.5

NT = N // P
G = D // 512
K_LEAD = 5
Q_LEAD = 3
V_BLOCKS = 5
LAST = H - 1
VIA_S = frozenset()
Q_GAP = 1
EARLY = False
NEG_ON_S = True
PAIR_K = True
ACC0_ON_S = False
C_LAG = 2
WARM = 4
WARM2 = 0


def tile_esmcontactheadapc_d1p_kernel(
    tc, x_bytes, x_scale, w_q_words, w_q_scales, g_q, w_k_words, w_k_scales, w_head, b_head, out
):
    nc = tc.nc
    with ExitStack() as ctx:
        keep = ctx.enter_context(tc.tile_pool(name="keep", bufs=1))
        work = ctx.enter_context(tc.tile_pool(name="work", bufs=3))
        psum = ctx.enter_context(tc.psum_pool(name="psum", bufs=2))

        def bank(tag):
            t = psum.tile([P, 512], F32, name="bank_" + tag, tag=tag, bufs={"q": 2, "k": 2, "sc": 3, "cs": 1}[tag])
            return t

        def kept(name, shape, dt):
            t = keep.tile(shape, dt, name=name, tag=name, align_bytes=64)
            return t

        zero = kept("zero", [P, N], BF16)
        nc.vector.memset(zero[:], 0.0)
        dummy = kept("dummy", [P, 1], F32)
        nc.scalar.activation(out=dummy[:], in_=zero[:, 0:1], func=ACT.Exp)

        def warm(count):
            for c in range(count):
                nc.tensor.matmul(bank("sc")[:], lhsT=zero[:, 0:P], rhs=zero[:], start=True, stop=True)

        warm(WARM)
        x8 = [kept("x8_%d" % a, [P, D], U8) for a in range(NT)]
        xs = kept("xs", [P, NT, 8], F32)
        nc.sync.dma_start(out=xs[:], in_=x_scale.rearrange("(a p) j -> p a j", p=P))
        for a in range(NT):
            nc.sync.dma_start(out=x8[a][:], in_=x_bytes[P * a : P * (a + 1), :])
        g_rows = kept("g_rows", [P, E], BF16)
        w_b = kept("w_b", [P, H], BF16)
        b_b = kept("b_b", [P, 1], BF16)
        nc.gpsimd.memset(g_rows[:], 0.0)
        nc.gpsimd.dma_start(out=g_rows[0:H, :], in_=g_q.rearrange("(h c) -> h c", h=H))
        ident = kept("ident", [P, P], F32)
        make_identity(nc, ident[:])
        nc.gpsimd.dma_start(out=w_b[:], in_=w_head.partition_broadcast(P))
        nc.gpsimd.dma_start(out=b_b[:], in_=b_head.partition_broadcast(P))
        raw_s = {}
        raw_w = {}
        words = {"q": w_q_words, "k": w_k_words}
        scales = {"q": w_q_scales, "k": w_k_scales}
        for w in ("k", "q"):
            raw_s[w] = kept("raw_s_" + w, [P, G, H * E], U8)
            nc.vector.memset(raw_s[w][:].bitcast(I32), 0)
            for hp in range(2):
                raw_w[w, hp] = kept("raw_w_%s%d" % (w, hp), [P, G, 2048], U8)

        def load_scales(w):
            for s in range(4):
                nc.sync.dma_start(
                    out=raw_s[w][32 * s : 32 * s + 4].bitcast(I32),
                    in_=scales[w].bitcast(I32)[:, 4 * s : 4 * s + 4, :].rearrange("g s c -> s g c"),
                )

        def load_words(w, hp):
            nc.sync.dma_start(
                out=raw_w[w, hp][:].bitcast(I32),
                in_=words[w].bitcast(I32)[:, :, 512 * hp : 512 * hp + 512].rearrange("g p c -> p g c"),
            )

        load_scales("k")
        load_words("k", 0)
        load_scales("q")
        load_words("q", 0)
        load_words("k", 1)
        load_words("q", 1)

        r_cols = kept("r_cols", [P, NT, P], F32)
        nc.gpsimd.memset(r_cols[:], 0.0)
        z_lhs = kept("z_lhs", [P, NT, P], F32)
        nc.gpsimd.memset(z_lhs[:], 0.0)

        perm_w = {}
        perm_s = {}

        def permute_scales(w):
            perm_s[w] = kept("perm_s_" + w, [P, G * H * E], U8)
            nc.vector.tensor_copy(
                out=perm_s[w][:].bitcast(I32).rearrange("p (t q b) -> p t q b", t=4, b=2),
                in_=raw_s[w][:].rearrange("p g c -> p (g c)").bitcast(I32).rearrange("p (q t b) -> p t q b", t=4, b=2),
            )

        def permute_words(w, hp):
            perm_w[w, hp] = kept("perm_w_%s%d" % (w, hp), [P, G * 2048], U8)
            nc.vector.tensor_copy(
                out=perm_w[w, hp][:].bitcast(I32).rearrange("p (t q b) -> p t q b", t=4, b=4),
                in_=raw_w[w, hp][:].rearrange("p g c -> p (g c)").bitcast(I32).rearrange("p (q t b) -> p t q b", t=4, b=4),
            )

        xb = [kept("xb_%d" % a, [P, D], BF16) for a in range(NT)]
        xt = [kept("xt_%d" % a, [P, G, P, 4], BF16) for a in range(NT)]
        xq = [kept("xq_%d" % a, [P, G * P], U32) for a in range(NT)]
        xq_s = [kept("xqs_%d" % a, [P, G * P], U8) for a in range(NT)]

        def widen(a):
            for c in range(8):
                cols = slice(P * c, P * (c + 1))
                src = x8[a][:, cols].bitcast(F8)
                if c < V_BLOCKS:
                    nc.vector.tensor_scalar(
                        out=xb[a][:, cols], in0=src, scalar1=xs[:, a, c : c + 1], scalar2=None, op0=MULT
                    )
                else:
                    nc.scalar.activation(out=xb[a][:, cols], in_=src, func=ACT.Copy, scale=xs[:, a, c : c + 1])

        def turn(a):
            ps = bank("q" if a % 2 == 0 else "k")
            w32 = xb[a][:].bitcast(F32)
            for g in range(G):
                for u in range(2):
                    s = 2 * g + u
                    nc.tensor.transpose(
                        ps[:, P * s : P * (s + 1)], w32[:, 256 * g + u : 256 * (g + 1) : 2], ident[:]
                    )
            warm(WARM2)
            return ps

        def turned_out(a, ps):
            nc.scalar.copy(
                out=xt[a][:].rearrange("p g r t -> p (g r t)").bitcast(F32).rearrange("p (g r u) -> p g r u", g=G, u=2),
                in_=ps[:].rearrange("p (g u r) -> p g r u", g=G, u=2),
            )

        def quant_x(a):
            nc.vector.quantize_mx(
                out=xq[a][:].bitcast(F8X4), scales=xq_s[a][:], in_=xt[a][:].rearrange("p g r t -> p (g r t)")
            )

        g_perm = kept("g_perm", [P, 4, P], F32)
        g_cols = kept("g_cols", [P, H, 4], F32)

        def gain_rows():
            nc.vector.tensor_copy(
                out=g_perm[:].rearrange("p t (q b) -> p t q b", b=8),
                in_=g_rows[:].rearrange("p (q t b) -> p t q b", t=4, b=8),
            )

        def gain_columns():
            psg = bank("sc")
            for t in range(4):
                nc.tensor.transpose(psg[:, P * t : P * (t + 1)], g_perm[:, t, :], ident[:])
            nc.vector.tensor_copy(out=g_cols[:], in_=psg[:].rearrange("p (t m) -> p m t", t=4)[:, 0:H, :])

        w512 = kept("w512", [P, H], F32)
        w_pick = kept("w_pick", [P, H], F32)
        one_col = kept("one_col", [P, 1], F32)
        w_col = kept("w_col", [P, 1], F32)
        w_half = kept("w_half", [P, 1], F32)

        def head_weights():
            nc.vector.tensor_scalar(out=w512[:], in0=w_b[:], scalar1=float(N), scalar2=None, op0=MULT)
            nc.vector.tensor_tensor(out=w_pick[:], in0=ident[:, 0:H], in1=w_b[:], op=MULT)
            nc.vector.tensor_reduce(out=one_col[:], in_=ident[:, 0:H], axis=X, op=ADD)
            nc.vector.tensor_reduce(out=w_col[:], in_=w_pick[:], axis=X, op=ADD)
            nc.vector.tensor_scalar(out=w_half[:], in0=w_col[:], scalar1=-0.5, scalar2=None, op0=MULT)

        widen(0)
        widen(1)
        ps0 = turn(0)
        turned_out(0, ps0)
        widen(2)
        ps1 = turn(1)
        turned_out(1, ps1)
        quant_x(0)
        widen(3)
        permute_scales("k")
        quant_x(1)
        permute_words("k", 0)
        ps2 = turn(2)
        turned_out(2, ps2)
        ps3 = turn(3)
        turned_out(3, ps3)
        quant_x(2)
        quant_x(3)
        permute_scales("q")
        gain_rows()
        permute_words("q", 0)

        unit_ps = {}
        raw = {}
        codes = {}
        plane = {}

        def project(w, m):
            h, nb = divmod(m, NT)
            hp, hh = divmod(h, 2)
            ps = bank(w)
            unit_ps[w, m] = ps
            for t in range(4):
                for g in range(G):
                    o = t * 1024 + g * 512 + hh * 256
                    so = t * 1024 + g * 512 + h * 128
                    nc.tensor.matmul_mx(
                        out=ps[:, P * t : P * (t + 1)],
                        lhsT=perm_w[w, hp][:, o : o + 256].bitcast(F4X4),
                        lhsT_scale=perm_s[w][:, so : so + P],
                        rhs=xq[nb][:, P * g : P * (g + 1)].bitcast(F8X4),
                        rhs_scale=xq_s[nb][:, P * g : P * (g + 1)],
                        start=(g == 0),
                        stop=(g == G - 1),
                    )

        def copy_q(m):
            h = m // NT
            r = work.tile([P, P, 4], BF16, name="q_raw", tag="q_raw", bufs=3, align_bytes=64)
            raw["q", m] = r
            if m in VIA_S:
                flat = work.tile([P, 4, P], BF16, name="q_flat", tag="q_flat", bufs=2, align_bytes=64)
                for t in range(4):
                    nc.scalar.activation(
                        out=flat[:, t, :],
                        in_=unit_ps["q", m][:, P * t : P * (t + 1)],
                        func=ACT.Copy,
                        scale=g_cols[:, h, t : t + 1],
                    )
                flat_q[m] = flat
                return
            nc.vector.tensor_tensor(
                out=r[:],
                in0=unit_ps["q", m][:].rearrange("p (t n) -> p n t", t=4),
                in1=g_cols[:, h, :].unsqueeze(1).to_broadcast([P, P, 4]),
                op=MULT,
            )

        flat_q = {}

        def interleave_q(m):
            if m in VIA_S:
                nc.vector.tensor_copy(out=raw["q", m][:], in_=flat_q[m][:].rearrange("p t n -> p n t"))

        def copy_k(m):
            if PAIR_K:
                if m % 2 == 0:
                    pair = work.tile([P, 2 * P, 4], BF16, name="k_raw", tag="k_raw", bufs=2, align_bytes=64)
                    raw["k", m] = pair
                else:
                    raw["k", m] = raw["k", m - 1]
                half = P * (m % 2)
                nc.scalar.copy(
                    out=raw["k", m][:, half : half + P, :], in_=unit_ps["k", m][:].rearrange("p (t n) -> p n t", t=4)
                )
                return
            r = work.tile([P, P, 4], BF16, name="k_raw", tag="k_raw", bufs=3, align_bytes=64)
            raw["k", m] = r
            nc.scalar.copy(out=r[:], in_=unit_ps["k", m][:].rearrange("p (t n) -> p n t", t=4))

        def quant(w, m):
            h, nb = divmod(m, NT)
            if w == "k" and PAIR_K and nb % 2 == 0:
                return
            if nb == (1 if w == "k" and PAIR_K else 0):
                c = work.tile([P, N], U32, name="codes_" + w, tag="codes_" + w, bufs=3, align_bytes=64)
                s = work.tile([P, N], U8, name="plane_" + w, tag="plane_" + w, bufs=3, align_bytes=64)
                codes[w, h] = c
                plane[w, h] = s
            cols = slice(P * nb, P * (nb + 1))
            if w == "k" and PAIR_K:
                cols = slice(P * (nb - 1), P * (nb + 1))
            nc.vector.quantize_mx(
                out=codes[w, h][:, cols].bitcast(F8X4),
                scales=plane[w, h][:, cols],
                in_=raw[w, m][:].rearrange("p n t -> p (n t)"),
            )

        sc = {}
        bias = {}
        e_of = {}
        z_of = {}
        rz = {}
        coef = {}
        a_of = {}
        acc = [kept("acc_%d" % i, [P, N], F32) for i in range(NT)]
        col_ps = {}

        def score(n):
            h, i = divmod(n, NT)
            ps = bank("sc")
            sc[n] = ps
            cols = slice(P * i, P * (i + 1))
            nc.tensor.matmul_mx(
                out=ps[:],
                lhsT=codes["q", h][:, cols].bitcast(F8X4),
                lhsT_scale=plane["q", h][:, cols],
                rhs=codes["k", h][:].bitcast(F8X4),
                rhs_scale=plane["k", h][:],
                start=True,
                stop=True,
            )

        def row_max(n):
            b = work.tile([P, 1], F32, name="bias", tag="bias", bufs=4)
            bias[n] = b
            if NEG_ON_S:
                mx = work.tile([P, 1], F32, name="mx", tag="mx", bufs=4)
                nc.vector.tensor_reduce(out=mx[:], in_=sc[n][:], axis=X, op=MAX)
                mx_of[n] = mx
                return
            trash = work.tile([P, N], BF16, name="trash", tag="trash", bufs=1)
            nc.vector.tensor_scalar(
                out=trash[:], in0=sc[n][:], scalar1=-SCALE, scalar2=None, op0=MULT, op1=MIN, accum_out=b[:]
            )

        mx_of = {}

        def bias_of(n):
            if NEG_ON_S:
                nc.scalar.activation(out=bias[n][:], in_=mx_of[n][:], func=ACT.Copy, scale=-SCALE)

        def expo(n):
            e = work.tile([P, N], F32, name="e", tag="e", bufs=4)
            z = work.tile([P, 1], F32, name="z", tag="z", bufs=4)
            e_of[n] = e
            z_of[n] = z
            nc.scalar.activation(out=e[:], in_=sc[n][:], func=ACT.Exp, bias=bias[n][:], scale=SCALE, accum_out=z[:])

        def recip(n):
            h, i = divmod(n, NT)
            if h == LAST:
                r = z_lhs[:, i, h : h + 1]
            else:
                r_tile = work.tile([P, 1], F32, name="rz", tag="rz", bufs=4)
                r = r_tile[:]
            rz[n] = r
            nc.vector.reciprocal(out=r, in_=z_of[n][:])
            if h == LAST:
                c = work.tile([P, 1], F32, name="coef", tag="coef", bufs=4)
                coef[n] = c
                nc.gpsimd.tensor_tensor(out=c[:], in0=r, in1=w512[:, h : h + 1], op=MULT)

        def norm(n):
            if n // NT == LAST:
                return
            a = work.tile([P, N], F32, name="a", tag="a", bufs=4)
            a_of[n] = a
            nc.scalar.activation(out=a[:], in_=e_of[n][:], func=ACT.Copy, scale=rz[n])

        def accumulate(n):
            h, i = divmod(n, NT)
            if h == 0:
                if ACC0_ON_S:
                    nc.scalar.activation(out=acc[i][:], in_=a_of[n][:], func=ACT.Copy, scale=w512[:, 0:1])
                else:
                    nc.vector.tensor_scalar(out=acc[i][:], in0=a_of[n][:], scalar1=w512[:, 0:1], scalar2=None, op0=MULT)
            else:
                nc.vector.scalar_tensor_tensor(
                    out=acc[i][:],
                    in0=(e_of if h == LAST else a_of)[n][:],
                    scalar=coef[n][:] if h == LAST else w512[:, h : h + 1],
                    in1=acc[i][:],
                    op0=MULT,
                    op1=ADD,
                )

        def transpose_add(dst, src, start, stop):
            nc.tensor.matmul(dst, lhsT=src, rhs=ident[:], is_transpose=True, start=start, stop=stop)

        def col_sums(n):
            h, i = divmod(n, NT)
            if i == 0:
                col_ps[h] = bank("cs")
            for j in range(NT):
                cols = slice(P * j, P * (j + 1))
                transpose_add(col_ps[h][:, cols], a_of[n][:, cols], i == 0 and j == 0, i == NT - 1 and j == NT - 1)

        def col_reduce(h):
            nc.vector.tensor_reduce(
                out=r_cols[:, :, h], in_=col_ps[h][:].rearrange("p (j i) -> p j i", j=NT), axis=X, op=ADD
            )

        def col_sums_last(n):
            i = n % NT
            if i == 0:
                col_ps[LAST] = bank("cs")
            nc.tensor.matmul(col_ps[LAST][:], lhsT=z_lhs[:, i, :], rhs=e_of[n][:], start=(i == 0), stop=(i == NT - 1))
            if i == 0:
                for j in range(NT):
                    transpose_add(col_ps[LAST][:, P * j : P * (j + 1)], r_cols[:, j, :], False, False)

        tiles = H * NT
        for n in range(-K_LEAD, tiles + 1):
            if 0 <= n + K_LEAD < tiles:
                project("k", n + K_LEAD)
            if n == -4:
                gain_columns()
            if n == -3:
                head_weights()
            if 0 <= n + Q_LEAD < tiles:
                project("q", n + Q_LEAD)
            if 0 <= n < tiles:
                row_max(n)
            if 0 <= n - 1 < tiles:
                recip(n - 1)
            if 0 <= n + K_LEAD - 1 < tiles:
                copy_k(n + K_LEAD - 1)
            if 0 <= n < tiles:
                bias_of(n)
            if 0 <= n - 1 < tiles:
                norm(n - 1)
            if 0 <= n + Q_LEAD - 1 < tiles:
                copy_q(n + Q_LEAD - 1)
            if 0 <= n < tiles:
                expo(n)
            if 0 <= n + Q_LEAD - Q_GAP < tiles:
                interleave_q(n + Q_LEAD - Q_GAP)
            if 0 <= n + K_LEAD - 1 < tiles:
                quant("k", n + K_LEAD - 1)
            if 0 <= n + Q_LEAD - Q_GAP < tiles:
                quant("q", n + Q_LEAD - Q_GAP)
            if n == -2:
                permute_words("k", 1)
            if n == 1:
                permute_words("q", 1)
            if 0 <= n - C_LAG < LAST * NT:
                col_sums(n - C_LAG)
                if (n - C_LAG) % NT == NT - 1:
                    col_reduce((n - C_LAG) // NT)
            if 0 <= n + 1 < tiles:
                score(n + 1)
            if n == tiles - 2:
                col_sums_last(n - 2)
            if n >= tiles - 2:
                col_sums_last(n - 1)
            if 0 <= n - 1 < tiles:
                accumulate(n - 1)

        dummy2 = kept("dummy2", [P, 1], F32)
        nc.scalar.activation(out=dummy2[:], in_=z_of[tiles - 1][:], func=ACT.Sigmoid)
        r_row = kept("r_row", [P, N], F32)
        wr_row = kept("wr_row", [P, N], F32)
        nc.vector.tensor_scalar(out=r_row[:], in0=col_ps[LAST][:], scalar1=one_col[:], scalar2=None, op0=ADD)
        for part in (slice(0, P), slice(P, N)):
            nc.vector.tensor_scalar(out=wr_row[:, part], in0=r_row[:, part], scalar1=w_half[:], scalar2=None, op0=MULT)
        po = [bank("q" if i % 2 == 0 else "k") for i in range(NT)]
        for i in range(NT):
            for j in range(i, NT):
                transpose_add(po[i][:, P * j : P * (j + 1)], acc[j][:, P * i : P * (i + 1)], j == i, False)
        sg = [kept("sg_%d" % i, [P, N], F32) for i in range(NT)]
        mirror = {}
        for i in range(1, NT):
            mirror[i] = bank("sc")
        for i in range(NT):
            rows = slice(P * i, P * (i + 1))
            right = slice(P * i, N)
            nc.tensor.matmul(po[i][:, right], lhsT=wr_row[:, rows], rhs=r_row[:, right], start=False, stop=True)
        for i in range(NT):
            rows = slice(P * i, P * (i + 1))
            right = slice(P * i, N)
            lg = work.tile([P, N], F32, name="lg", tag="lg", bufs=4)
            nc.vector.tensor_tensor(out=lg[:, right], in0=po[i][:, right], in1=acc[i][:, right], op=ADD)
            nc.scalar.activation(out=sg[i][:, right], in_=lg[:, right], func=ACT.Sigmoid, bias=b_b[:], scale=1.0)
            for j in range(i + 1, NT):
                nc.tensor.transpose(mirror[j][:, rows], sg[i][:, P * j : P * (j + 1)], ident[:])
            if i > 0:
                nc.vector.tensor_copy(out=sg[i][:, 0 : P * i], in_=mirror[i][:, 0 : P * i])
            nc.sync.dma_start(out=out[rows, :], in_=sg[i][:])
